import numpy as np, ml_dtypes
CORES = [32,40,48,56,64,72,80,88,96,104,112,120]
N = 12
KB, QP = 2, 32
def setup_inputs(rng):
    q = rng.standard_normal((N, 128, QP), dtype=np.float32) / 4; k = rng.standard_normal((N, 128, KB * 128), dtype=np.float32)
    a = 2 * np.pi * rng.random((N, QP)); s = 400 * rng.random((N, QP)) ** 1.5; q[:, 0, :] = s * np.cos(a); q[:, 1, :] = s * np.sin(a); q[:, 2, :] = 150 * rng.standard_normal((N, QP)); k[:, 2, :] = 1 + k[:, 2, :] / 50
    a = (2 * np.pi * rng.random() + np.pi / 2 * (rng.permutation(N).reshape(N, 1, 1) + 0.5) / N - 0.5 + (np.arange(KB).reshape(1, KB, 1) + rng.random((N, KB, 128))) / KB).reshape(N, KB * 128); k[:, 0, :] = np.cos(a); k[:, 1, :] = np.sin(a)
    return {"q": q.astype(ml_dtypes.bfloat16), "k": k.astype(ml_dtypes.bfloat16), "v": rng.standard_normal((N, 128, KB * 128), dtype=np.float32).astype(ml_dtypes.bfloat16)}
def setup_inputs_big(rng):
    d = setup_inputs(rng)
    for k in ("v",): d[k] = (d[k].astype(np.float32) * 1048576.0).astype(d[k].dtype)
    return d
def setup_inputs_small(rng):
    d = setup_inputs(rng)
    for k in ("v",): d[k] = (d[k].astype(np.float32) * (1 / 1048576.0)).astype(d[k].dtype)
    return d
def reference(q, k, v):
    Q, K, V = q.astype(np.float64), k.astype(np.float64), v.astype(np.float64)
    y = np.zeros((N, QP, 128))
    for r in range(N):
        js = list(range(N))
        S = np.concatenate([K[j].T @ Q[r] for j in js], axis=0)
        P = np.exp(S - S.max(axis=0)); P = P / P.sum(axis=0)
        y[r] = P.T @ np.concatenate([V[j][:, 128 * b:128 * b + 128] for j in js for b in range(KB)], axis=0)
    return {"y": y.astype(ml_dtypes.bfloat16)}

@@ -1,0 +1,342 @@
+import numpy as np
+from concourse.bass import DstId, RemoteDMATransfer
+from concourse.mybir import dt, AluOpType, AxisListType, ActivationFunctionType
+
+NPORT = 3
+NPLAIN = 2
+NDIRECT = 1
+QP = 32
+SLOT = 40
+MSG = 34
+BIG = 30000.0
+
+SCRATCH = {
+    "qd": ("dram", [128, 32], "bfloat16"),
+    "qs": ("sbuf", [128, 128], "bfloat16"),
+    "ks": ("sbuf", [128, 256], "bfloat16"),
+    "vs": ("sbuf", [128, 256], "bfloat16"),
+    "ones": ("sbuf", [128, 128], "bfloat16"),
+    "ident": ("sbuf", [128, 128], "bfloat16"),
+    "R": ("sbuf", [128, 128], "bfloat16"),
+    "maskG": ("sbuf", [128, 4], "float32"),
+    "negm": ("sbuf", [128, 1], "bfloat16"),
+    "lsum": ("sbuf", [128, 1], "float32"),
+    "P": ("sbuf", [128, 256], "bfloat16"),
+    "X": ("sbuf", [128, 8], "bfloat16"),
+    "PTs0": ("sbuf", [128, 128], "bfloat16"),
+    "PTs1": ("sbuf", [128, 128], "bfloat16"),
+    "msg": ("sbuf", [128, 160], "bfloat16"),
+    "land": ("sbuf", [128, 480], "bfloat16"),
+    "Sel": ("sbuf", [128, 32], "bfloat16"),
+    "pm": ("sbuf", [128, 12], "float32"),
+    "minnm": ("sbuf", [128, 1], "float32"),
+    "nmm": ("sbuf", [128, 12], "float32"),
+    "wm": ("sbuf", [128, 12], "float32"),
+    "wcol": ("sbuf", [128, 4], "float32"),
+    "wl": ("sbuf", [128, 12], "bfloat16"),
+    "OTs0": ("sbuf", [128, 128], "bfloat16"),
+    "OTs1": ("sbuf", [128, 128], "bfloat16"),
+    "OTs2": ("sbuf", [128, 128], "bfloat16"),
+    "OTs3": ("sbuf", [128, 128], "bfloat16"),
+    "den": ("sbuf", [128, 1], "float32"),
+    "rden": ("sbuf", [128, 1], "float32"),
+    "ysb": ("sbuf", [128, 128], "bfloat16"),
+    "pS": ("psum", [128, 512], "float32"),
+    "pST": ("psum", [128, 512], "float32"),
+    "pO": ("psum", [128, 512], "float32"),
+    "pY": ("psum", [128, 512], "float32"),
+    "pT0": ("psum", [128, 1024], "bfloat16"),
+    "pT1": ("psum", [128, 1024], "bfloat16"),
+    "pT2": ("psum", [128, 1024], "bfloat16"),
+    "pT3": ("psum", [128, 1024], "bfloat16"),
+}
+SEMAPHORES = ["qdl", "qown", "kin", "vin", "qdin", "qin", "res", "sent", "stored"] + ["e%d" % i for i in range(48)]
+
+
+def _bits(mask):
+    return [b for b in range(mask.bit_length()) if (mask >> b) & 1]
+
+
+def _mk(engines):
+    m = 0
+    for b in engines:
+        m |= 1 << b
+    return m
+
+
+def _chunks(lst, n):
+    out, at = [], 0
+    for i in range(n):
+        ln = (len(lst) - at + (n - i) - 1) // (n - i)
+        out.append(lst[at:at + ln])
+        at += ln
+    return out
+
+
+def _plan(T, topo):
+    cores = list(T.cores)
+    n = len(cores)
+    allc = range(topo.CHIPS * topo.CORES_PER_CHIP)
+    plan = []
+    for j, c0 in enumerate(cores):
+        ch = topo.chip(c0)
+        order = sorted([r for r in range(n) if r != j], key=lambda r: (r - j) % n)
+        same = [r for r in order if topo.same_plane(topo.chip(cores[r]), ch)]
+        cross = [r for r in order if r not in same]
+        others = sorted([c for c in allc if topo.chip(c) == ch and c != c0],
+                        key=lambda c: (topo.die(c) != topo.die(c0), c))
+        ports = [c for c in others if all(topo.may_write(c, cores[r]) for r in cross)][:NPORT]
+        plains = [c for c in others if c not in ports][:NPLAIN]
+        groups = [(c0, same[:NDIRECT])]
+        groups += list(zip(plains, _chunks(same[NDIRECT:], NPLAIN)))
+        groups += list(zip(ports, _chunks(cross, NPORT)))
+        plan.append({"c0": c0, "helpers": plains + ports, "groups": groups})
+    where = {}
+    for j in range(n):
+        for c, ranks in plan[j]["groups"]:
+            lst = ([j] if c == plan[j]["c0"] else []) + list(ranks)
+            for gi, r in enumerate(lst):
+                where[(j, r)] = (c, gi, len([x for x in lst if x != j]))
+    return plan, where
+
+
+def _per(nmsg, neng):
+    p = 1
+    while p * 2 * nmsg <= neng:
+        p *= 2
+    return p
+
+
+def rank_program(g, core, T, topo):
+    plan, where = _plan(T, topo)
+    cores = list(T.cores)
+    n = len(cores)
+    j = None
+    for r in range(n):
+        if topo.chip(cores[r]) == topo.chip(core):
+            j = r
+    if j is None:
+        return
+    mine = [ranks for c, ranks in plan[j]["groups"] if c == core]
+    if not mine:
+        return
+    partners = list(mine[0])
+    c0 = plan[j]["c0"]
+    is_rank = core == c0
+    helpers = plan[j]["helpers"]
+    served = ([j] if is_rank else []) + partners
+    G = len(served)
+    nq = QP * G
+
+    PE, DVE, ACT, SP = g.tensor, g.vector, g.scalar, g.sync
+    A, F, AX = AluOpType, ActivationFunctionType, AxisListType.X
+    S = T.sem
+    cnt = [0]
+
+    def ev():
+        s = S["e%d" % cnt[0]]
+        cnt[0] += 1
+        return s
+
+    def did(c):
+        rid, pid, _se = topo.addr(c)
+        return DstId(rid=rid, pnc=pid)
+
+    sent = [0]
+
+    def fused(transfers):
+        g.remote_dma_fused(transfers, local_sem=S.sent)
+        for t, ne in transfers_eng:
+            sent[0] += ne
+        del transfers_eng[:]
+
+    transfers_eng = []
+
+    def tr(src, dsts, dcs, engines, sem):
+        t = RemoteDMATransfer(dst_ids=[did(c) for c in dcs], dma_engine_mask=_mk(engines), remote_sem=sem,
+                              srcs=[src], dsts=dsts)
+        transfers_eng.append((t, len(engines)))
+        return t
+
+    off = _bits(topo.mask(core, cores[partners[0]]))
+    on = _bits(topo.mask(core, helpers[0] if is_rank else c0))
+    hi = [e for e in on if e not in off]
+
+    if is_rank:
+        SP.dma_start(T.qd[:], T.q[:]).then_inc(S.qdl, 16)
+        ACT.dma_start(T.ks[:], T.k[:]).then_inc(S.kin, 16)
+        SP.dma_start(T.vs[:], T.v[:]).then_inc(S.vin, 16)
+        ACT.dma_start(T.qs[:, 0:QP], T.q[:]).then_inc(S.qown, 16)
+
+    e_z, e_one, e_id, e_R = ev(), ev(), ev(), ev()
+    DVE.memset(T.R[:], 0.0).then_inc(e_z, 1)
+    if is_rank:
+        e_land, e_z12 = ev(), ev()
+        DVE.memset(T.ones[:], 1.0).then_inc(e_one, 1)
+        DVE.memset(T.land[:], 0.0).then_inc(e_land, 1)
+        DVE.memset(T.pm[:], 0.0).then_inc(e_z12, 1)
+    else:
+        ACT.wait_ge(e_z, 1)
+        ACT.activation(T.ones[:], T.R[:], F.Exp).then_inc(e_one, 1)
+    g.wait_ge(e_one, 1)
+    g.affine_select(T.ident[:], T.ones[:], [[-1, 128]], A.is_equal, 0.0, 0, 1).then_inc(e_id, 1)
+    DVE.wait_ge(e_z, 1)
+    DVE.wait_ge(e_id, 1)
+    nR = 0
+    for gi in range(G):
+        p0 = QP * gi
+        for s in range(3):
+            DVE.tensor_copy(T.R[p0:p0 + QP, SLOT * s:SLOT * s + QP], T.ident[p0:p0 + QP, p0:p0 + QP]).then_inc(e_R, 1)
+            nR += 1
+        DVE.tensor_reduce(T.maskG[0:nq, gi:gi + 1], T.ident[0:nq, p0:p0 + QP], AX, A.add).then_inc(e_R, 1)
+        nR += 1
+    PE.wait_ge(e_id, 1)
+    PE.wait_ge(e_R, nR)
+    DVE.wait_ge(e_R, nR)
+    if is_rank:
+        e_selp, e_sel = ev(), ev()
+        PE.matmul(T.pY[0:128, 0:QP], T.R[0:QP, 0:128], T.ident[0:QP, 0:QP], True, True).then_inc(e_selp, 1)
+        DVE.wait_ge(e_selp, 1)
+        DVE.tensor_copy(T.Sel[:], T.pY[0:128, 0:QP]).then_inc(e_sel, 1)
+
+    def q_targets():
+        dcs, dsts = [], []
+        for t in partners:
+            c, gi, _n = where[(t, j)]
+            dcs.append(c)
+            dsts.append(T.qs[:, QP * gi:QP * gi + QP])
+        return dcs, dsts
+
+    dcs, dsts = q_targets()
+    if is_rank:
+        g.wait_ge(e_land, 1)
+        g.wait_ge(S.qdl, 16)
+        fused([tr(T.qd[:], [T.qd[:] for _ in helpers], helpers, hi, S.qdin),
+               tr(T.qd[:], dsts, dcs, off, S.qin)])
+        g.wait_ge(S.kin, 16)
+        fused([tr(T.ks[:], [T.ks[:] for _ in helpers], helpers, on, S.kin)])
+        g.wait_ge(S.vin, 16)
+        fused([tr(T.vs[:], [T.vs[:] for _ in helpers], helpers, on, S.vin)])
+        e_pm1, e_pm = ev(), ev()
+        g.wait_ge(e_z12, 1)
+        g.affine_select(T.pm[:], T.pm[:], [[0, 4], [-SLOT, 3]], A.is_ge, BIG, 0, 1).then_inc(e_pm1, 1)
+        g.wait_ge(e_pm1, 1)
+        g.affine_select(T.pm[:], T.pm[:], [[0, 4], [SLOT, 3]], A.is_ge, BIG, SLOT - 1, -1).then_inc(e_pm, 1)
+    else:
+        g.wait_ge(S.qdin, len(hi))
+        fused([tr(T.qd[:], dsts, dcs, off, S.qin)])
+
+    e_S, e_M, e_P, e_X, e_T0, e_T1, e_C0, e_C1, e_ST, e_O = [ev() for _ in range(10)]
+    e_own, e_msg = ev(), ev()
+    if is_rank:
+        PE.wait_ge(S.qown, 16)
+    PE.wait_ge(S.qin, len(off) * len(partners))
+    PE.wait_ge(S.kin, len(on))
+    PE.matmul(T.pS[0:nq, 0:256], T.qs[:, 0:nq], T.ks[:], True, True).then_inc(e_S, 1)
+    DVE.wait_ge(e_S, 1)
+    DVE.tensor_reduce(T.negm[0:nq, :], T.pS[0:nq, 0:256], AX, A.max, negate=True).then_inc(e_M, 1)
+    ACT.wait_ge(e_M, 1)
+    ACT.activation(T.P[0:nq, :], T.pS[0:nq, 0:256], F.Exp, bias=T.negm[0:nq, :],
+                   accum_out=T.lsum[0:nq, :]).then_inc(e_P, 1)
+    DVE.wait_ge(e_M, 1)
+    DVE.tensor_scalar(T.X[0:nq, 0:2 * G:2], T.maskG[0:nq, 0:G], T.negm[0:nq, :], None, A.mult).then_inc(e_X, 1)
+    DVE.wait_ge(e_P, 1)
+    DVE.tensor_scalar(T.X[0:nq, 1:2 * G:2], T.maskG[0:nq, 0:G], T.lsum[0:nq, :], None, A.mult).then_inc(e_X, 1)
+    PE.wait_ge(e_P, 1)
+    PE.transpose(T.pT0[0:128, 0:nq], T.P[0:nq, 0:128], T.ident[0:nq, 0:nq]).then_inc(e_T0, 1)
+    PE.transpose(T.pT1[0:128, 0:nq], T.P[0:nq, 128:256], T.ident[0:nq, 0:nq]).then_inc(e_T1, 1)
+    PE.wait_ge(e_X, 2)
+    PE.matmul(T.pST[0:128, 0:2 * G], T.R[0:nq, 0:128], T.X[0:nq, 0:2 * G], True, True).then_inc(e_ST, 1)
+    DVE.wait_ge(e_T0, 1)
+    DVE.tensor_copy(T.PTs0[:, 0:nq], T.pT0[0:128, 0:nq]).then_inc(e_C0, 1)
+    ACT.wait_ge(e_T1, 1)
+    ACT.activation(T.PTs1[:, 0:nq], T.pT1[0:128, 0:nq], F.Copy).then_inc(e_C1, 1)
+    PE.wait_ge(S.vin, len(on))
+    PE.wait_ge(e_C0, 1)
+    PE.matmul(T.pO[0:128, 0:nq], T.vs[:, 0:128], T.PTs0[:, 0:nq], True, False)
+    PE.wait_ge(e_C1, 1)
+    PE.matmul(T.pO[0:128, 0:nq], T.vs[:, 128:256], T.PTs1[:, 0:nq], False, True).then_inc(e_O, 1)
+
+    def out_ap(gi, a, b):
+        if served[gi] == j:
+            return T.land[:, SLOT * j + a:SLOT * j + b], e_own
+        return T.msg[:, SLOT * gi + a:SLOT * gi + b], e_msg
+
+    DVE.wait_ge(e_ST, 1)
+    order = [gi for gi in range(G) if served[gi] != j] + [gi for gi in range(G) if served[gi] == j]
+    for gi in order:
+        ap, e = out_ap(gi, QP, MSG)
+        DVE.tensor_copy(ap, T.pST[0:128, 2 * gi:2 * gi + 2]).then_inc(e, 1)
+    DVE.wait_ge(e_O, 1)
+    for gi in order:
+        ap, e = out_ap(gi, 0, QP)
+        DVE.tensor_copy(ap, T.pO[0:128, QP * gi:QP * gi + QP]).then_inc(e, 1)
+
+    per = _per(len(partners), len(off))
+    g.wait_ge(e_msg, 2 * len(partners))
+    trs, at = [], 0
+    for gi in range(G):
+        r = served[gi]
+        if r == j:
+            continue
+        trs.append(tr(T.msg[:, SLOT * gi:SLOT * gi + MSG], [T.land[:, SLOT * j:SLOT * j + MSG]], [cores[r]],
+                      off[at:at + per], S.res))
+        at += per
+    fused(trs)
+    g.wait_ge(S.sent, sent[0])
+    if not is_rank:
+        return
+
+    total = 0
+    for t in range(n):
+        if t != j:
+            total += _per(where[(t, j)][2], len(off))
+    pT = [T.pT0, T.pT1, T.pT2, T.pT3]
+    OTs = [T.OTs0, T.OTs1, T.OTs2, T.OTs3]
+    W = 3 * SLOT
+    e_TR = [ev() for _ in range(4)]
+    e_sc = [ev() for _ in range(4)]
+    e_min, e_nmm, e_W, e_wl, e_DEN, e_den, e_rden, e_Y, e_ys = [ev() for _ in range(9)]
+    nm12 = T.land[:, QP:12 * SLOT:SLOT]
+    l12 = T.land[:, QP + 1:12 * SLOT:SLOT]
+
+    PE.wait_ge(S.res, total)
+    PE.wait_ge(e_own, 2)
+    for a in range(4):
+        PE.transpose(pT[a][0:W, 0:128], T.land[:, W * a:W * a + W], T.ident[:]).then_inc(e_TR[a], 1)
+    DVE.wait_ge(S.res, total)
+    DVE.wait_ge(e_own, 2)
+    DVE.wait_ge(e_pm, 1)
+    DVE.tensor_reduce(T.minnm[:], nm12, AX, A.min).then_inc(e_min, 1)
+    DVE.tensor_tensor(T.nmm[:], nm12, T.pm[:], A.add).then_inc(e_nmm, 1)
+    ACT.wait_ge(e_min, 1)
+    ACT.wait_ge(e_nmm, 1)
+    for a in range(4):
+        ACT.activation(T.wm[:, 3 * a:3 * a + 3], T.nmm[:, 3 * a:3 * a + 3], F.Exp, bias=T.minnm[:], scale=-1.0,
+                       accum_out=T.wcol[:, a:a + 1]).then_inc(e_W, 1)
+    DVE.wait_ge(e_W, 4)
+    ACT.wait_ge(e_W, 4)
+    DVE.tensor_tensor(T.wl[:], T.wm[:], l12, A.mult).then_inc(e_wl, 1)
+    for a in (0, 1):
+        DVE.wait_ge(e_TR[a], 1)
+        DVE.tensor_scalar(OTs[a][0:W, :], pT[a][0:W, 0:128], T.wcol[0:W, a:a + 1], None, A.mult).then_inc(e_sc[a], 1)
+    for a in (2, 3):
+        ACT.wait_ge(e_TR[a], 1)
+        ACT.activation(OTs[a][0:W, :], pT[a][0:W, 0:128], F.Copy, scale=T.wcol[0:W, a:a + 1]).then_inc(e_sc[a], 1)
+    PE.wait_ge(e_sel, 1)
+    PE.wait_ge(e_wl, 1)
+    PE.matmul(T.pST[0:QP, 0:12], T.Sel[:], T.wl[:], True, True).then_inc(e_DEN, 1)
+    for i, a in enumerate((0, 2, 1, 3)):
+        PE.wait_ge(e_sc[a], 1)
+        mm = PE.matmul(T.pY[0:QP, 0:128], T.Sel[0:W, :], OTs[a][0:W, :], i == 0, i == 3)
+    mm.then_inc(e_Y, 1)
+    DVE.wait_ge(e_DEN, 1)
+    DVE.tensor_reduce(T.den[0:QP, :], T.pST[0:QP, 0:12], AX, A.add).then_inc(e_den, 1)
+    DVE.wait_ge(e_den, 1)
+    DVE.reciprocal(T.rden[0:QP, :], T.den[0:QP, :]).then_inc(e_rden, 1)
+    DVE.wait_ge(e_rden, 1)
+    DVE.wait_ge(e_Y, 1)
+    DVE.tensor_scalar(T.ysb[0:QP, :], T.pY[0:QP, 0:128], T.rden[0:QP, :], None, A.mult).then_inc(e_ys, 1)
+    SP.wait_ge(e_ys, 1)
+    SP.dma_start(T.y[:], T.ysb[0:QP, :]).then_inc(S.stored, 16)
+    SP.wait_ge(S.stored, 16)

@@ -17,6 +17,7 @@ SCRATCH = {
     "vs": ("sbuf", [128, 256], "bfloat16"),
     "ones": ("sbuf", [128, 128], "bfloat16"),
     "ident": ("sbuf", [128, 128], "bfloat16"),
+    "cb": ("sbuf", [128, 128], "bfloat16"),
     "R": ("sbuf", [128, 128], "bfloat16"),
     "maskG": ("sbuf", [128, 4], "float32"),
     "negm": ("sbuf", [128, 1], "bfloat16"),
@@ -50,7 +51,8 @@ SCRATCH = {
     "pT2": ("psum", [128, 1024], "bfloat16"),
     "pT3": ("psum", [128, 1024], "bfloat16"),
 }
-SEMAPHORES = ["qdl", "qown", "kin", "vin", "qdin", "qin", "res", "sent", "stored"] + ["e%d" % i for i in range(48)]
+SEMAPHORES = ["qdl", "qown", "kin", "vin", "qdin", "qin", "res", "sent", "stored", "cst", "mk"] + \
+             ["e%d" % i for i in range(48)]
 
 
 def _bits(mask):
@@ -143,24 +145,22 @@ def rank_program(g, core, T, topo):
         return DstId(rid=rid, pnc=pid)
 
     sent = [0]
+    pending = []
+
+    def tr(src, dsts, dcs, engines, sem):
+        pending.append(len(engines))
+        return RemoteDMATransfer(dst_ids=[did(c) for c in dcs], dma_engine_mask=_mk(engines), remote_sem=sem,
+                                 srcs=[src], dsts=dsts)
 
     def fused(transfers):
         g.remote_dma_fused(transfers, local_sem=S.sent)
-        for t, ne in transfers_eng:
-            sent[0] += ne
-        del transfers_eng[:]
-
-    transfers_eng = []
-
-    def tr(src, dsts, dcs, engines, sem):
-        t = RemoteDMATransfer(dst_ids=[did(c) for c in dcs], dma_engine_mask=_mk(engines), remote_sem=sem,
-                              srcs=[src], dsts=dsts)
-        transfers_eng.append((t, len(engines)))
-        return t
+        sent[0] += sum(pending)
+        del pending[:]
 
     off = _bits(topo.mask(core, cores[partners[0]]))
     on = _bits(topo.mask(core, helpers[0] if is_rank else c0))
     hi = [e for e in on if e not in off]
+    ncst = len(off) * len(helpers)
 
     if is_rank:
         SP.dma_start(T.qd[:], T.q[:]).then_inc(S.qdl, 16)
@@ -168,60 +168,83 @@ def rank_program(g, core, T, topo):
         SP.dma_start(T.vs[:], T.v[:]).then_inc(S.vin, 16)
         ACT.dma_start(T.qs[:, 0:QP], T.q[:]).then_inc(S.qown, 16)
 
-    e_z, e_one, e_id, e_R = ev(), ev(), ev(), ev()
-    DVE.memset(T.R[:], 0.0).then_inc(e_z, 1)
     if is_rank:
-        e_land, e_z12 = ev(), ev()
-        DVE.memset(T.ones[:], 1.0).then_inc(e_one, 1)
+        e_m0, e_m1, e_land = ev(), ev(), ev()
+        DVE.memset(T.maskG[:], 0.0).then_inc(e_m0, 1)
+        DVE.wait_ge(e_m0, 1)
+        for gi in range(4):
+            DVE.memset(T.maskG[QP * gi:QP * gi + QP, gi:gi + 1], 1.0).then_inc(e_m1, 1)
         DVE.memset(T.land[:], 0.0).then_inc(e_land, 1)
-        DVE.memset(T.pm[:], 0.0).then_inc(e_z12, 1)
+        g.wait_ge(e_m1, 4)
+        fused([tr(T.maskG[:], [T.maskG[:] for _ in helpers], helpers, on, S.mk)])
+        DVE.wait_ge(e_m1, 4)
+        DVE.wait_ge(e_land, 1)
+        PE.wait_ge(S.cst, ncst)
+        DVE.wait_ge(S.cst, ncst)
     else:
+        piece = helpers.index(core)
+        e_cz, e_c = ev(), ev()
+        if piece == 4:
+            DVE.memset(T.pm[:], 0.0).then_inc(e_cz, 1)
+        else:
+            DVE.memset(T.cb[:], 0.0).then_inc(e_cz, 1)
+        g.wait_ge(e_cz, 1)
+        if piece in (0, 1):
+            src, dst = T.cb[:, 0:64], T.ident[:, 64 * piece:64 * piece + 64]
+            g.affine_select(src, src, [[-1, 64]], A.not_equal, 1.0, -64 * piece, 1).then_inc(e_c, 1)
+            nc = 1
+        elif piece == 2:
+            src, dst = T.cb[:], T.R[:]
+            for gi in range(2):
+                ap = T.cb[QP * gi:QP * gi + QP, 0:3 * SLOT]
+                g.affine_select(ap, ap, [[0, 3], [-1, SLOT]], A.not_equal, 1.0, 0, 1).then_inc(e_c, 1)
+            nc = 2
+        elif piece == 3:
+            src, dst = T.cb[:, 0:QP], T.Sel[:]
+            for s in range(3):
+                g.affine_select(src, src, [[-1, QP]], A.not_equal, 1.0, -SLOT * s, 1).then_inc(e_c, 1)
+                g.wait_ge(e_c, s + 1)
+            nc = 3
+        else:
+            src, dst = T.pm[:], T.pm[:]
+            g.affine_select(src, src, [[0, 4], [-SLOT, 3]], A.is_ge, BIG, 0, 1).then_inc(e_c, 1)
+            g.wait_ge(e_c, 1)
+            g.affine_select(src, src, [[0, 4], [SLOT, 3]], A.is_ge, BIG, SLOT - 1, -1).then_inc(e_c, 1)
+            nc = 2
+        g.wait_ge(e_c, nc)
+        fused([tr(src, [dst], [c0], off, S.cst)])
+        e_z, e_one, e_id, e_R = ev(), ev(), ev(), ev()
+        DVE.memset(T.R[:], 0.0).then_inc(e_z, 1)
         ACT.wait_ge(e_z, 1)
         ACT.activation(T.ones[:], T.R[:], F.Exp).then_inc(e_one, 1)
-    g.wait_ge(e_one, 1)
-    g.affine_select(T.ident[:], T.ones[:], [[-1, 128]], A.is_equal, 0.0, 0, 1).then_inc(e_id, 1)
-    DVE.wait_ge(e_z, 1)
-    DVE.wait_ge(e_id, 1)
-    nR = 0
-    for gi in range(G):
-        p0 = QP * gi
-        for s in range(3):
-            DVE.tensor_copy(T.R[p0:p0 + QP, SLOT * s:SLOT * s + QP], T.ident[p0:p0 + QP, p0:p0 + QP]).then_inc(e_R, 1)
-            nR += 1
-        DVE.tensor_reduce(T.maskG[0:nq, gi:gi + 1], T.ident[0:nq, p0:p0 + QP], AX, A.add).then_inc(e_R, 1)
-        nR += 1
-    PE.wait_ge(e_id, 1)
-    PE.wait_ge(e_R, nR)
-    DVE.wait_ge(e_R, nR)
-    if is_rank:
-        e_selp, e_sel = ev(), ev()
-        PE.matmul(T.pY[0:128, 0:QP], T.R[0:QP, 0:128], T.ident[0:QP, 0:QP], True, True).then_inc(e_selp, 1)
-        DVE.wait_ge(e_selp, 1)
-        DVE.tensor_copy(T.Sel[:], T.pY[0:128, 0:QP]).then_inc(e_sel, 1)
+        g.wait_ge(e_one, 1)
+        g.affine_select(T.ident[:], T.ones[:], [[-1, 128]], A.is_equal, 0.0, 0, 1).then_inc(e_id, 1)
+        DVE.wait_ge(e_z, 1)
+        DVE.wait_ge(e_id, 1)
+        nR = 0
+        for gi in range(G):
+            p0 = QP * gi
+            for s in range(3):
+                DVE.tensor_copy(T.R[p0:p0 + QP, SLOT * s:SLOT * s + QP],
+                                T.ident[p0:p0 + QP, p0:p0 + QP]).then_inc(e_R, 1)
+                nR += 1
+        PE.wait_ge(e_id, 1)
+        PE.wait_ge(e_R, nR)
+        DVE.wait_ge(S.mk, len(on))
 
-    def q_targets():
-        dcs, dsts = [], []
-        for t in partners:
-            c, gi, _n = where[(t, j)]
-            dcs.append(c)
-            dsts.append(T.qs[:, QP * gi:QP * gi + QP])
-        return dcs, dsts
-
-    dcs, dsts = q_targets()
+    dcs, dsts = [], []
+    for t in partners:
+        c, gi, _n = where[(t, j)]
+        dcs.append(c)
+        dsts.append(T.qs[:, QP * gi:QP * gi + QP])
     if is_rank:
         g.wait_ge(e_land, 1)
         g.wait_ge(S.qdl, 16)
         fused([tr(T.qd[:], [T.qd[:] for _ in helpers], helpers, hi, S.qdin),
                tr(T.qd[:], dsts, dcs, off, S.qin)])
-        g.wait_ge(S.kin, 16)
-        fused([tr(T.ks[:], [T.ks[:] for _ in helpers], helpers, on, S.kin)])
-        g.wait_ge(S.vin, 16)
-        fused([tr(T.vs[:], [T.vs[:] for _ in helpers], helpers, on, S.vin)])
-        e_pm1, e_pm = ev(), ev()
-        g.wait_ge(e_z12, 1)
-        g.affine_select(T.pm[:], T.pm[:], [[0, 4], [-SLOT, 3]], A.is_ge, BIG, 0, 1).then_inc(e_pm1, 1)
-        g.wait_ge(e_pm1, 1)
-        g.affine_select(T.pm[:], T.pm[:], [[0, 4], [SLOT, 3]], A.is_ge, BIG, SLOT - 1, -1).then_inc(e_pm, 1)
+        for buf, sem in ((T.ks, S.kin), (T.vs, S.vin)):
+            g.wait_ge(sem, 16)
+            fused([tr(buf[:], [buf[:] for _ in helpers], helpers, on, sem)])
     else:
         g.wait_ge(S.qdin, len(hi))
         fused([tr(T.qd[:], dsts, dcs, off, S.qin)])
@@ -296,7 +319,8 @@ def rank_program(g, core, T, topo):
     W = 3 * SLOT
     e_TR = [ev() for _ in range(4)]
     e_sc = [ev() for _ in range(4)]
-    e_min, e_nmm, e_W, e_wl, e_DEN, e_den, e_rden, e_Y, e_ys = [ev() for _ in range(9)]
+    e_W = [ev() for _ in range(4)]
+    e_min, e_nmm, e_wl, e_DEN, e_den, e_rden, e_Y, e_ys = [ev() for _ in range(8)]
     nm12 = T.land[:, QP:12 * SLOT:SLOT]
     l12 = T.land[:, QP + 1:12 * SLOT:SLOT]
 
@@ -306,29 +330,28 @@ def rank_program(g, core, T, topo):
         PE.transpose(pT[a][0:W, 0:128], T.land[:, W * a:W * a + W], T.ident[:]).then_inc(e_TR[a], 1)
     DVE.wait_ge(S.res, total)
     DVE.wait_ge(e_own, 2)
-    DVE.wait_ge(e_pm, 1)
     DVE.tensor_reduce(T.minnm[:], nm12, AX, A.min).then_inc(e_min, 1)
     DVE.tensor_tensor(T.nmm[:], nm12, T.pm[:], A.add).then_inc(e_nmm, 1)
     ACT.wait_ge(e_min, 1)
     ACT.wait_ge(e_nmm, 1)
     for a in range(4):
         ACT.activation(T.wm[:, 3 * a:3 * a + 3], T.nmm[:, 3 * a:3 * a + 3], F.Exp, bias=T.minnm[:], scale=-1.0,
-                       accum_out=T.wcol[:, a:a + 1]).then_inc(e_W, 1)
-    DVE.wait_ge(e_W, 4)
-    ACT.wait_ge(e_W, 4)
-    DVE.tensor_tensor(T.wl[:], T.wm[:], l12, A.mult).then_inc(e_wl, 1)
-    for a in (0, 1):
+                       accum_out=T.wcol[:, a:a + 1]).then_inc(e_W[a], 1)
+    for a in (0, 1, 2):
+        DVE.wait_ge(e_W[a], 1)
         DVE.wait_ge(e_TR[a], 1)
         DVE.tensor_scalar(OTs[a][0:W, :], pT[a][0:W, 0:128], T.wcol[0:W, a:a + 1], None, A.mult).then_inc(e_sc[a], 1)
-    for a in (2, 3):
-        ACT.wait_ge(e_TR[a], 1)
-        ACT.activation(OTs[a][0:W, :], pT[a][0:W, 0:128], F.Copy, scale=T.wcol[0:W, a:a + 1]).then_inc(e_sc[a], 1)
-    PE.wait_ge(e_sel, 1)
-    PE.wait_ge(e_wl, 1)
-    PE.matmul(T.pST[0:QP, 0:12], T.Sel[:], T.wl[:], True, True).then_inc(e_DEN, 1)
-    for i, a in enumerate((0, 2, 1, 3)):
+    DVE.wait_ge(e_W[3], 1)
+    DVE.tensor_tensor(T.wl[:], T.wm[:], l12, A.mult).then_inc(e_wl, 1)
+    ACT.wait_ge(e_W[3], 1)
+    ACT.wait_ge(e_TR[3], 1)
+    ACT.activation(OTs[3][0:W, :], pT[3][0:W, 0:128], F.Copy, scale=T.wcol[0:W, 3:4]).then_inc(e_sc[3], 1)
+    for a in range(4):
         PE.wait_ge(e_sc[a], 1)
-        mm = PE.matmul(T.pY[0:QP, 0:128], T.Sel[0:W, :], OTs[a][0:W, :], i == 0, i == 3)
+        mm = PE.matmul(T.pY[0:QP, 0:128], T.Sel[0:W, :], OTs[a][0:W, :], a == 0, a == 3)
+        if a == 1:
+            PE.wait_ge(e_wl, 1)
+            PE.matmul(T.pST[0:QP, 0:12], T.Sel[:], T.wl[:], True, True).then_inc(e_DEN, 1)
     mm.then_inc(e_Y, 1)
     DVE.wait_ge(e_DEN, 1)
     DVE.tensor_reduce(T.den[0:QP, :], T.pST[0:QP, 0:12], AX, A.add).then_inc(e_den, 1)

@@ -2,9 +2,6 @@ import numpy as np
 from concourse.bass import DstId, RemoteDMATransfer
 from concourse.mybir import dt, AluOpType, AxisListType, ActivationFunctionType
 
-NPORT = 3
-NPLAIN = 2
-NDIRECT = 1
 QP = 32
 SLOT = 40
 MSG = 34
@@ -20,6 +17,8 @@ SCRATCH = {
     "cb": ("sbuf", [128, 128], "bfloat16"),
     "R": ("sbuf", [128, 128], "bfloat16"),
     "maskG": ("sbuf", [128, 4], "float32"),
+    "mneg": ("sbuf", [128, 4], "float32"),
+    "maskR": ("sbuf", [128, 4], "float32"),
     "negm": ("sbuf", [128, 1], "bfloat16"),
     "lsum": ("sbuf", [128, 1], "float32"),
     "P": ("sbuf", [128, 256], "bfloat16"),
@@ -29,12 +28,15 @@ SCRATCH = {
     "msg": ("sbuf", [128, 160], "bfloat16"),
     "land": ("sbuf", [128, 480], "bfloat16"),
     "Sel": ("sbuf", [128, 32], "bfloat16"),
+    "Ws0": ("sbuf", [128, 32], "bfloat16"),
+    "Ws1": ("sbuf", [128, 32], "bfloat16"),
     "pm": ("sbuf", [128, 12], "float32"),
     "minnm": ("sbuf", [128, 1], "float32"),
     "nmm": ("sbuf", [128, 12], "float32"),
     "wm": ("sbuf", [128, 12], "float32"),
+    "w12": ("sbuf", [128, 12], "float32"),
     "wcol": ("sbuf", [128, 4], "float32"),
-    "wl": ("sbuf", [128, 12], "bfloat16"),
+    "wl": ("sbuf", [128, 12], "float32"),
     "OTs0": ("sbuf", [128, 128], "bfloat16"),
     "OTs1": ("sbuf", [128, 128], "bfloat16"),
     "OTs2": ("sbuf", [128, 128], "bfloat16"),
@@ -51,8 +53,8 @@ SCRATCH = {
     "pT2": ("psum", [128, 1024], "bfloat16"),
     "pT3": ("psum", [128, 1024], "bfloat16"),
 }
-SEMAPHORES = ["qdl", "qown", "kin", "vin", "qdin", "qin", "res", "sent", "stored", "cst", "mk"] + \
-             ["e%d" % i for i in range(48)]
+SEMAPHORES = ["qdl", "qown", "kin", "vin", "qdin", "qin", "res0", "res1", "res2", "res3", "sent", "stored", "cst",
+              "mk"] + ["e%d" % i for i in range(64)]
 
 
 def _bits(mask):
@@ -66,20 +68,11 @@ def _mk(engines):
     return m
 
 
-def _chunks(lst, n):
-    out, at = [], 0
-    for i in range(n):
-        ln = (len(lst) - at + (n - i) - 1) // (n - i)
-        out.append(lst[at:at + ln])
-        at += ln
-    return out
-
-
 def _plan(T, topo):
     cores = list(T.cores)
     n = len(cores)
     allc = range(topo.CHIPS * topo.CORES_PER_CHIP)
-    plan = []
+    plan, pos = [], {}
     for j, c0 in enumerate(cores):
         ch = topo.chip(c0)
         order = sorted([r for r in range(n) if r != j], key=lambda r: (r - j) % n)
@@ -87,19 +80,23 @@ def _plan(T, topo):
         cross = [r for r in order if r not in same]
         others = sorted([c for c in allc if topo.chip(c) == ch and c != c0],
                         key=lambda c: (topo.die(c) != topo.die(c0), c))
-        ports = [c for c in others if all(topo.may_write(c, cores[r]) for r in cross)][:NPORT]
-        plains = [c for c in others if c not in ports][:NPLAIN]
-        groups = [(c0, same[:NDIRECT])]
-        groups += list(zip(plains, _chunks(same[NDIRECT:], NPLAIN)))
-        groups += list(zip(ports, _chunks(cross, NPORT)))
-        plan.append({"c0": c0, "helpers": plains + ports, "groups": groups})
+        ports = [c for c in others if all(topo.may_write(c, cores[r]) for r in cross)]
+        plains = [c for c in others if c not in ports]
+        carry = {c0: same[0:2], plains[0]: same[2:3], plains[1]: same[3:4], plains[2]: same[4:5],
+                 ports[0]: cross[0:2], ports[1]: cross[2:4], ports[2]: cross[4:5], ports[3]: cross[5:6]}
+        serve = {c0: [j, same[3], same[4]], plains[0]: [same[2]], plains[1]: [same[1]], plains[2]: [same[0]],
+                 ports[0]: [cross[4]], ports[1]: [cross[2]], ports[2]: [cross[0], cross[1]],
+                 ports[3]: [cross[3], cross[5]]}
+        plan.append({"c0": c0, "helpers": ports + plains, "carry": carry, "serve": serve})
+        due = [j] + same + sorted(cross, key=lambda r: not topo.mates(topo.chip(cores[r]), ch))
+        for i, t in enumerate(due):
+            pos[(j, t)] = i
     where = {}
     for j in range(n):
-        for c, ranks in plan[j]["groups"]:
-            lst = ([j] if c == plan[j]["c0"] else []) + list(ranks)
+        for c, lst in plan[j]["serve"].items():
             for gi, r in enumerate(lst):
                 where[(j, r)] = (c, gi, len([x for x in lst if x != j]))
-    return plan, where
+    return plan, where, pos
 
 
 def _per(nmsg, neng):
@@ -110,7 +107,7 @@ def _per(nmsg, neng):
 
 
 def rank_program(g, core, T, topo):
-    plan, where = _plan(T, topo)
+    plan, where, pos = _plan(T, topo)
     cores = list(T.cores)
     n = len(cores)
     j = None
@@ -119,14 +116,14 @@ def rank_program(g, core, T, topo):
             j = r
     if j is None:
         return
-    mine = [ranks for c, ranks in plan[j]["groups"] if c == core]
-    if not mine:
+    if core not in plan[j]["carry"]:
         return
-    partners = list(mine[0])
+    carry = list(plan[j]["carry"][core])
+    served = list(plan[j]["serve"][core])
     c0 = plan[j]["c0"]
     is_rank = core == c0
     helpers = plan[j]["helpers"]
-    served = ([j] if is_rank else []) + partners
+    guests = [r for r in served if r != j]
     G = len(served)
     nq = QP * G
 
@@ -157,7 +154,7 @@ def rank_program(g, core, T, topo):
         sent[0] += sum(pending)
         del pending[:]
 
-    off = _bits(topo.mask(core, cores[partners[0]]))
+    off = _bits(topo.mask(core, cores[carry[0]]))
     on = _bits(topo.mask(core, helpers[0] if is_rank else c0))
     hi = [e for e in on if e not in off]
     ncst = len(off) * len(helpers)
@@ -179,27 +176,35 @@ def rank_program(g, core, T, topo):
         fused([tr(T.maskG[:], [T.maskG[:] for _ in helpers], helpers, on, S.mk)])
         DVE.wait_ge(e_m1, 4)
         DVE.wait_ge(e_land, 1)
+        e_p0, e_p1, e_pm = ev(), ev(), ev()
+        DVE.memset(T.mneg[:], -BIG).then_inc(e_p0, 1)
+        DVE.wait_ge(e_p0, 1)
+        for gi in range(4):
+            DVE.memset(T.mneg[QP * gi:QP * gi + QP, gi:gi + 1], 0.0).then_inc(e_p1, 1)
+        ACT.wait_ge(e_p1, 4)
+        ACT.activation(T.maskR[:], T.mneg[:], F.Exp).then_inc(e_pm, 1)
+        DVE.wait_ge(e_pm, 1)
         PE.wait_ge(S.cst, ncst)
         DVE.wait_ge(S.cst, ncst)
     else:
         piece = helpers.index(core)
         e_cz, e_c = ev(), ev()
-        if piece == 4:
+        if piece == 6:
             DVE.memset(T.pm[:], 0.0).then_inc(e_cz, 1)
         else:
             DVE.memset(T.cb[:], 0.0).then_inc(e_cz, 1)
         g.wait_ge(e_cz, 1)
-        if piece in (0, 1):
-            src, dst = T.cb[:, 0:64], T.ident[:, 64 * piece:64 * piece + 64]
-            g.affine_select(src, src, [[-1, 64]], A.not_equal, 1.0, -64 * piece, 1).then_inc(e_c, 1)
+        if piece < 4:
+            src, dst = T.cb[:, 0:QP], T.ident[:, QP * piece:QP * piece + QP]
+            g.affine_select(src, src, [[-1, QP]], A.not_equal, 1.0, -QP * piece, 1).then_inc(e_c, 1)
             nc = 1
-        elif piece == 2:
+        elif piece == 4:
             src, dst = T.cb[:], T.R[:]
-            for gi in range(2):
+            for gi in range(3):
                 ap = T.cb[QP * gi:QP * gi + QP, 0:3 * SLOT]
                 g.affine_select(ap, ap, [[0, 3], [-1, SLOT]], A.not_equal, 1.0, 0, 1).then_inc(e_c, 1)
-            nc = 2
-        elif piece == 3:
+            nc = 3
+        elif piece == 5:
             src, dst = T.cb[:, 0:QP], T.Sel[:]
             for s in range(3):
                 g.affine_select(src, src, [[-1, QP]], A.not_equal, 1.0, -SLOT * s, 1).then_inc(e_c, 1)
@@ -233,7 +238,7 @@ def rank_program(g, core, T, topo):
         DVE.wait_ge(S.mk, len(on))
 
     dcs, dsts = [], []
-    for t in partners:
+    for t in carry:
         c, gi, _n = where[(t, j)]
         dcs.append(c)
         dsts.append(T.qs[:, QP * gi:QP * gi + QP])
@@ -251,9 +256,10 @@ def rank_program(g, core, T, topo):
 
     e_S, e_M, e_P, e_X, e_T0, e_T1, e_C0, e_C1, e_ST, e_O = [ev() for _ in range(10)]
     e_own, e_msg = ev(), ev()
+    mask = T.maskR if is_rank else T.maskG
     if is_rank:
         PE.wait_ge(S.qown, 16)
-    PE.wait_ge(S.qin, len(off) * len(partners))
+    PE.wait_ge(S.qin, len(off) * len(guests))
     PE.wait_ge(S.kin, len(on))
     PE.matmul(T.pS[0:nq, 0:256], T.qs[:, 0:nq], T.ks[:], True, True).then_inc(e_S, 1)
     DVE.wait_ge(e_S, 1)
@@ -262,14 +268,13 @@ def rank_program(g, core, T, topo):
     ACT.activation(T.P[0:nq, :], T.pS[0:nq, 0:256], F.Exp, bias=T.negm[0:nq, :],
                    accum_out=T.lsum[0:nq, :]).then_inc(e_P, 1)
     DVE.wait_ge(e_M, 1)
-    DVE.tensor_scalar(T.X[0:nq, 0:2 * G:2], T.maskG[0:nq, 0:G], T.negm[0:nq, :], None, A.mult).then_inc(e_X, 1)
+    DVE.tensor_scalar(T.X[0:nq, 0:2 * G:2], mask[0:nq, 0:G], T.negm[0:nq, :], None, A.mult).then_inc(e_X, 1)
     DVE.wait_ge(e_P, 1)
-    DVE.tensor_scalar(T.X[0:nq, 1:2 * G:2], T.maskG[0:nq, 0:G], T.lsum[0:nq, :], None, A.mult).then_inc(e_X, 1)
+    DVE.tensor_scalar(T.X[0:nq, 1:2 * G:2], mask[0:nq, 0:G], T.lsum[0:nq, :], None, A.mult).then_inc(e_X, 1)
+    PE.wait_ge(e_M, 1)
     PE.wait_ge(e_P, 1)
     PE.transpose(T.pT0[0:128, 0:nq], T.P[0:nq, 0:128], T.ident[0:nq, 0:nq]).then_inc(e_T0, 1)
     PE.transpose(T.pT1[0:128, 0:nq], T.P[0:nq, 128:256], T.ident[0:nq, 0:nq]).then_inc(e_T1, 1)
-    PE.wait_ge(e_X, 2)
-    PE.matmul(T.pST[0:128, 0:2 * G], T.R[0:nq, 0:128], T.X[0:nq, 0:2 * G], True, True).then_inc(e_ST, 1)
     DVE.wait_ge(e_T0, 1)
     DVE.tensor_copy(T.PTs0[:, 0:nq], T.pT0[0:128, 0:nq]).then_inc(e_C0, 1)
     ACT.wait_ge(e_T1, 1)
@@ -279,87 +284,124 @@ def rank_program(g, core, T, topo):
     PE.matmul(T.pO[0:128, 0:nq], T.vs[:, 0:128], T.PTs0[:, 0:nq], True, False)
     PE.wait_ge(e_C1, 1)
     PE.matmul(T.pO[0:128, 0:nq], T.vs[:, 128:256], T.PTs1[:, 0:nq], False, True).then_inc(e_O, 1)
+    PE.wait_ge(e_X, 2)
+    PE.matmul(T.pST[0:128, 0:2 * G], T.R[0:nq, 0:128], T.X[0:nq, 0:2 * G], True, True).then_inc(e_ST, 1)
 
     def out_ap(gi, a, b):
         if served[gi] == j:
-            return T.land[:, SLOT * j + a:SLOT * j + b], e_own
+            at = SLOT * pos[(j, j)]
+            return T.land[:, at + a:at + b], e_own
         return T.msg[:, SLOT * gi + a:SLOT * gi + b], e_msg
 
-    DVE.wait_ge(e_ST, 1)
+    ACT.wait_ge(e_ST, 1)
     order = [gi for gi in range(G) if served[gi] != j] + [gi for gi in range(G) if served[gi] == j]
     for gi in order:
         ap, e = out_ap(gi, QP, MSG)
-        DVE.tensor_copy(ap, T.pST[0:128, 2 * gi:2 * gi + 2]).then_inc(e, 1)
+        ACT.activation(ap, T.pST[0:128, 2 * gi:2 * gi + 2], F.Copy).then_inc(e, 1)
     DVE.wait_ge(e_O, 1)
     for gi in order:
         ap, e = out_ap(gi, 0, QP)
         DVE.tensor_copy(ap, T.pO[0:128, QP * gi:QP * gi + QP]).then_inc(e, 1)
 
-    per = _per(len(partners), len(off))
-    g.wait_ge(e_msg, 2 * len(partners))
+    per = _per(len(guests), len(off))
+    g.wait_ge(e_msg, 2 * len(guests))
     trs, at = [], 0
     for gi in range(G):
         r = served[gi]
         if r == j:
             continue
-        trs.append(tr(T.msg[:, SLOT * gi:SLOT * gi + MSG], [T.land[:, SLOT * j:SLOT * j + MSG]], [cores[r]],
-                      off[at:at + per], S.res))
+        sl = pos[(r, j)]
+        trs.append(tr(T.msg[:, SLOT * gi:SLOT * gi + MSG], [T.land[:, SLOT * sl:SLOT * sl + MSG]], [cores[r]],
+                      off[at:at + per], S["res%d" % (sl // 3)]))
         at += per
     fused(trs)
     g.wait_ge(S.sent, sent[0])
     if not is_rank:
         return
 
-    total = 0
+    tot = [0, 0, 0, 0]
     for t in range(n):
         if t != j:
-            total += _per(where[(t, j)][2], len(off))
+            tot[pos[(j, t)] // 3] += _per(where[(t, j)][2], len(off))
+    res = [S["res%d" % a] for a in range(4)]
     pT = [T.pT0, T.pT1, T.pT2, T.pT3]
     OTs = [T.OTs0, T.OTs1, T.OTs2, T.OTs3]
+    Ws = [T.Ws0, T.Ws1]
+    pYh = [T.pY, T.pS]
     W = 3 * SLOT
+    H = 64
     e_TR = [ev() for _ in range(4)]
     e_sc = [ev() for _ in range(4)]
     e_W = [ev() for _ in range(4)]
-    e_min, e_nmm, e_wl, e_DEN, e_den, e_rden, e_Y, e_ys = [ev() for _ in range(8)]
+    e_ws = [ev() for _ in range(2)]
+    e_Y = [ev() for _ in range(2)]
+    e_min, e_n01, e_n23, e_w12, e_wl, e_den, e_rden, e_ys = [ev() for _ in range(8)]
     nm12 = T.land[:, QP:12 * SLOT:SLOT]
-    l12 = T.land[:, QP + 1:12 * SLOT:SLOT]
 
-    PE.wait_ge(S.res, total)
-    PE.wait_ge(e_own, 2)
     for a in range(4):
+        PE.wait_ge(res[a], tot[a])
+        if a == 0:
+            PE.wait_ge(e_own, 2)
         PE.transpose(pT[a][0:W, 0:128], T.land[:, W * a:W * a + W], T.ident[:]).then_inc(e_TR[a], 1)
-    DVE.wait_ge(S.res, total)
+    DVE.wait_ge(res[0], tot[0])
+    DVE.wait_ge(res[1], tot[1])
     DVE.wait_ge(e_own, 2)
+    DVE.tensor_tensor(T.nmm[:, 0:6], T.land[:, QP:6 * SLOT:SLOT], T.pm[:, 0:6], A.add).then_inc(e_n01, 1)
+    DVE.wait_ge(e_TR[0], 1)
+    DVE.tensor_copy(OTs[0][0:W, :], pT[0][0:W, 0:128]).then_inc(e_sc[0], 1)
+    ACT.wait_ge(e_TR[1], 1)
+    ACT.activation(OTs[1][0:W, :], pT[1][0:W, 0:128], F.Copy).then_inc(e_sc[1], 1)
+    DVE.wait_ge(res[2], tot[2])
+    DVE.wait_ge(res[3], tot[3])
     DVE.tensor_reduce(T.minnm[:], nm12, AX, A.min).then_inc(e_min, 1)
-    DVE.tensor_tensor(T.nmm[:], nm12, T.pm[:], A.add).then_inc(e_nmm, 1)
-    ACT.wait_ge(e_min, 1)
-    ACT.wait_ge(e_nmm, 1)
-    for a in range(4):
+    DVE.tensor_tensor(T.nmm[:, 6:12], T.land[:, 6 * SLOT + QP:12 * SLOT:SLOT], T.pm[:, 6:12], A.add).then_inc(e_n23, 1)
+
+    def wexp(a):
         ACT.activation(T.wm[:, 3 * a:3 * a + 3], T.nmm[:, 3 * a:3 * a + 3], F.Exp, bias=T.minnm[:], scale=-1.0,
                        accum_out=T.wcol[:, a:a + 1]).then_inc(e_W[a], 1)
-    for a in (0, 1, 2):
-        DVE.wait_ge(e_W[a], 1)
-        DVE.wait_ge(e_TR[a], 1)
-        DVE.tensor_scalar(OTs[a][0:W, :], pT[a][0:W, 0:128], T.wcol[0:W, a:a + 1], None, A.mult).then_inc(e_sc[a], 1)
-    DVE.wait_ge(e_W[3], 1)
-    DVE.tensor_tensor(T.wl[:], T.wm[:], l12, A.mult).then_inc(e_wl, 1)
-    ACT.wait_ge(e_W[3], 1)
-    ACT.wait_ge(e_TR[3], 1)
-    ACT.activation(OTs[3][0:W, :], pT[3][0:W, 0:128], F.Copy, scale=T.wcol[0:W, 3:4]).then_inc(e_sc[3], 1)
+
     for a in range(4):
-        PE.wait_ge(e_sc[a], 1)
-        mm = PE.matmul(T.pY[0:QP, 0:128], T.Sel[0:W, :], OTs[a][0:W, :], a == 0, a == 3)
-        if a == 1:
-            PE.wait_ge(e_wl, 1)
-            PE.matmul(T.pST[0:QP, 0:12], T.Sel[:], T.wl[:], True, True).then_inc(e_DEN, 1)
-    mm.then_inc(e_Y, 1)
-    DVE.wait_ge(e_DEN, 1)
-    DVE.tensor_reduce(T.den[0:QP, :], T.pST[0:QP, 0:12], AX, A.add).then_inc(e_den, 1)
+        ACT.wait_ge(res[a], tot[a])
+    ACT.wait_ge(e_own, 2)
+    ACT.wait_ge(e_min, 1)
+    ACT.wait_ge(e_n01, 1)
+    wexp(0)
+    ACT.activation(T.w12[0:QP, :], T.land[0:QP, QP:12 * SLOT:SLOT], F.Exp, bias=T.minnm[0:QP, :],
+                   scale=-1.0).then_inc(e_w12, 1)
+    wexp(1)
+    ACT.wait_ge(e_n23, 1)
+    wexp(2)
+    wexp(3)
+    for a in (0, 1):
+        DVE.wait_ge(e_W[a], 1)
+        DVE.tensor_scalar(Ws[a][0:W, :], T.Sel[0:W, :], T.wcol[0:W, a:a + 1], None, A.mult).then_inc(e_ws[a], 1)
+    for a in (2, 3):
+        ACT.wait_ge(e_W[a], 1)
+        ACT.wait_ge(e_TR[a], 1)
+        ACT.activation(OTs[a][0:W, :], pT[a][0:W, 0:128], F.Copy, scale=T.wcol[0:W, a:a + 1]).then_inc(e_sc[a], 1)
+    DVE.wait_ge(e_w12, 1)
+    DVE.tensor_tensor(T.wl[0:QP, :], T.w12[0:QP, :], T.land[0:QP, QP + 1:12 * SLOT:SLOT], A.mult).then_inc(e_wl, 1)
+    DVE.wait_ge(e_wl, 1)
+    DVE.tensor_reduce(T.den[0:QP, :], T.wl[0:QP, :], AX, A.add).then_inc(e_den, 1)
     DVE.wait_ge(e_den, 1)
     DVE.reciprocal(T.rden[0:QP, :], T.den[0:QP, :]).then_inc(e_rden, 1)
+    for a in range(4):
+        PE.wait_ge(e_sc[a], 1)
+        if a < 2:
+            PE.wait_ge(e_ws[a], 1)
+            lhs = Ws[a][0:W, :]
+        else:
+            lhs = T.Sel[0:W, :]
+        for h in range(2):
+            mm = PE.matmul(pYh[h][0:QP, 0:H], lhs, OTs[a][0:W, H * h:H * h + H], a == 0, a == 3)
+            if a == 3:
+                mm.then_inc(e_Y[h], 1)
     DVE.wait_ge(e_rden, 1)
-    DVE.wait_ge(e_Y, 1)
-    DVE.tensor_scalar(T.ysb[0:QP, :], T.pY[0:QP, 0:128], T.rden[0:QP, :], None, A.mult).then_inc(e_ys, 1)
-    SP.wait_ge(e_ys, 1)
+    DVE.wait_ge(e_Y[0], 1)
+    DVE.tensor_scalar(T.ysb[0:QP, 0:H], pYh[0][0:QP, 0:H], T.rden[0:QP, :], None, A.mult).then_inc(e_ys, 1)
+    ACT.wait_ge(e_rden, 1)
+    ACT.wait_ge(e_Y[1], 1)
+    ACT.activation(T.ysb[0:QP, H:2 * H], pYh[1][0:QP, 0:H], F.Copy, scale=T.rden[0:QP, :]).then_inc(e_ys, 1)
+    SP.wait_ge(e_ys, 2)
     SP.dma_start(T.y[:], T.ysb[0:QP, :]).then_inc(S.stored, 16)
     SP.wait_ge(S.stored, 16)

import numpy as np
from concourse.bass import DstId, RemoteDMATransfer
from concourse.mybir import dt, AluOpType, AxisListType, ActivationFunctionType

QP = 32
SLOT = 40
MSG = 34
BIG = 30000.0

SCRATCH = {
    "qd": ("dram", [128, 32], "bfloat16"),
    "qs": ("sbuf", [128, 128], "bfloat16"),
    "ks": ("sbuf", [128, 256], "bfloat16"),
    "vs": ("sbuf", [128, 256], "bfloat16"),
    "ones": ("sbuf", [128, 128], "bfloat16"),
    "ident": ("sbuf", [128, 128], "bfloat16"),
    "cb": ("sbuf", [128, 128], "bfloat16"),
    "R": ("sbuf", [128, 128], "bfloat16"),
    "maskG": ("sbuf", [128, 4], "float32"),
    "mneg": ("sbuf", [128, 4], "float32"),
    "maskR": ("sbuf", [128, 4], "float32"),
    "negm": ("sbuf", [128, 1], "bfloat16"),
    "lsum": ("sbuf", [128, 1], "float32"),
    "P": ("sbuf", [128, 256], "bfloat16"),
    "X": ("sbuf", [128, 8], "bfloat16"),
    "PTs0": ("sbuf", [128, 128], "bfloat16"),
    "PTs1": ("sbuf", [128, 128], "bfloat16"),
    "msg": ("sbuf", [128, 160], "bfloat16"),
    "land": ("sbuf", [128, 480], "bfloat16"),
    "Sel": ("sbuf", [128, 32], "bfloat16"),
    "Ws0": ("sbuf", [128, 32], "bfloat16"),
    "Ws1": ("sbuf", [128, 32], "bfloat16"),
    "pm": ("sbuf", [128, 12], "float32"),
    "minnm": ("sbuf", [128, 1], "float32"),
    "nmm": ("sbuf", [128, 12], "float32"),
    "wm": ("sbuf", [128, 12], "float32"),
    "w12": ("sbuf", [128, 12], "float32"),
    "wcol": ("sbuf", [128, 4], "float32"),
    "wl": ("sbuf", [128, 12], "float32"),
    "OTs0": ("sbuf", [128, 128], "bfloat16"),
    "OTs1": ("sbuf", [128, 128], "bfloat16"),
    "OTs2": ("sbuf", [128, 128], "bfloat16"),
    "OTs3": ("sbuf", [128, 128], "bfloat16"),
    "den": ("sbuf", [128, 1], "float32"),
    "rden": ("sbuf", [128, 1], "float32"),
    "ysb": ("sbuf", [128, 128], "bfloat16"),
    "pS": ("psum", [128, 512], "float32"),
    "pST": ("psum", [128, 512], "float32"),
    "pO": ("psum", [128, 512], "float32"),
    "pY": ("psum", [128, 512], "float32"),
    "pT0": ("psum", [128, 1024], "bfloat16"),
    "pT1": ("psum", [128, 1024], "bfloat16"),
    "pT2": ("psum", [128, 1024], "bfloat16"),
    "pT3": ("psum", [128, 1024], "bfloat16"),
}
SEMAPHORES = ["qdl", "qown", "kin", "vin", "qdin", "qin", "res0", "res1", "res2", "res3", "sent", "stored", "cst",
              "mk"] + ["e%d" % i for i in range(64)]


def _bits(mask):
    return [b for b in range(mask.bit_length()) if (mask >> b) & 1]


def _mk(engines):
    m = 0
    for b in engines:
        m |= 1 << b
    return m


def _plan(T, topo):
    cores = list(T.cores)
    n = len(cores)
    allc = range(topo.CHIPS * topo.CORES_PER_CHIP)
    plan, pos = [], {}
    for j, c0 in enumerate(cores):
        ch = topo.chip(c0)
        order = sorted([r for r in range(n) if r != j], key=lambda r: (r - j) % n)
        same = [r for r in order if topo.same_plane(topo.chip(cores[r]), ch)]
        cross = [r for r in order if r not in same]
        others = sorted([c for c in allc if topo.chip(c) == ch and c != c0],
                        key=lambda c: (topo.die(c) != topo.die(c0), c))
        ports = [c for c in others if all(topo.may_write(c, cores[r]) for r in cross)]
        plains = [c for c in others if c not in ports]
        carry = {c0: same[0:2], plains[0]: same[2:3], plains[1]: same[3:4], plains[2]: same[4:5],
                 ports[0]: cross[0:2], ports[1]: cross[2:4], ports[2]: cross[4:5], ports[3]: cross[5:6]}
        serve = {c0: [j, same[3], same[4]], plains[0]: [same[2]], plains[1]: [same[1]], plains[2]: [same[0]],
                 ports[0]: [cross[4]], ports[1]: [cross[2]], ports[2]: [cross[0], cross[1]],
                 ports[3]: [cross[3], cross[5]]}
        plan.append({"c0": c0, "helpers": ports + plains, "carry": carry, "serve": serve})
        due = [j] + same + sorted(cross, key=lambda r: not topo.mates(topo.chip(cores[r]), ch))
        for i, t in enumerate(due):
            pos[(j, t)] = i
    where = {}
    for j in range(n):
        for c, lst in plan[j]["serve"].items():
            for gi, r in enumerate(lst):
                where[(j, r)] = (c, gi, len([x for x in lst if x != j]))
    return plan, where, pos


def _per(nmsg, neng):
    p = 1
    while p * 2 * nmsg <= neng:
        p *= 2
    return p


def rank_program(g, core, T, topo):
    plan, where, pos = _plan(T, topo)
    cores = list(T.cores)
    n = len(cores)
    j = None
    for r in range(n):
        if topo.chip(cores[r]) == topo.chip(core):
            j = r
    if j is None:
        return
    if core not in plan[j]["carry"]:
        return
    carry = list(plan[j]["carry"][core])
    served = list(plan[j]["serve"][core])
    c0 = plan[j]["c0"]
    is_rank = core == c0
    helpers = plan[j]["helpers"]
    guests = [r for r in served if r != j]
    G = len(served)
    nq = QP * G

    PE, DVE, ACT, SP = g.tensor, g.vector, g.scalar, g.sync
    A, F, AX = AluOpType, ActivationFunctionType, AxisListType.X
    S = T.sem
    cnt = [0]

    def ev():
        s = S["e%d" % cnt[0]]
        cnt[0] += 1
        return s

    def did(c):
        rid, pid, _se = topo.addr(c)
        return DstId(rid=rid, pnc=pid)

    sent = [0]
    pending = []

    def tr(src, dsts, dcs, engines, sem):
        pending.append(len(engines))
        return RemoteDMATransfer(dst_ids=[did(c) for c in dcs], dma_engine_mask=_mk(engines), remote_sem=sem,
                                 srcs=[src], dsts=dsts)

    def fused(transfers):
        g.remote_dma_fused(transfers, local_sem=S.sent)
        sent[0] += sum(pending)
        del pending[:]

    off = _bits(topo.mask(core, cores[carry[0]]))
    on = _bits(topo.mask(core, helpers[0] if is_rank else c0))
    hi = [e for e in on if e not in off]
    ncst = len(off) * len(helpers)

    if is_rank:
        SP.dma_start(T.qd[:], T.q[:]).then_inc(S.qdl, 16)
        ACT.dma_start(T.ks[:], T.k[:]).then_inc(S.kin, 16)
        SP.dma_start(T.vs[:], T.v[:]).then_inc(S.vin, 16)
        ACT.dma_start(T.qs[:, 0:QP], T.q[:]).then_inc(S.qown, 16)

    if is_rank:
        e_m0, e_m1, e_land = ev(), ev(), ev()
        DVE.memset(T.maskG[:], 0.0).then_inc(e_m0, 1)
        DVE.wait_ge(e_m0, 1)
        for gi in range(4):
            DVE.memset(T.maskG[QP * gi:QP * gi + QP, gi:gi + 1], 1.0).then_inc(e_m1, 1)
        DVE.memset(T.land[:], 0.0).then_inc(e_land, 1)
        g.wait_ge(e_m1, 4)
        fused([tr(T.maskG[:], [T.maskG[:] for _ in helpers], helpers, on, S.mk)])
        DVE.wait_ge(e_m1, 4)
        DVE.wait_ge(e_land, 1)
        e_p0, e_p1, e_pm = ev(), ev(), ev()
        DVE.memset(T.mneg[:], -BIG).then_inc(e_p0, 1)
        DVE.wait_ge(e_p0, 1)
        for gi in range(4):
            DVE.memset(T.mneg[QP * gi:QP * gi + QP, gi:gi + 1], 0.0).then_inc(e_p1, 1)
        ACT.wait_ge(e_p1, 4)
        ACT.activation(T.maskR[:], T.mneg[:], F.Exp).then_inc(e_pm, 1)
        DVE.wait_ge(e_pm, 1)
        PE.wait_ge(S.cst, ncst)
        DVE.wait_ge(S.cst, ncst)
    else:
        piece = helpers.index(core)
        e_cz, e_c = ev(), ev()
        if piece == 6:
            DVE.memset(T.pm[:], 0.0).then_inc(e_cz, 1)
        else:
            DVE.memset(T.cb[:], 0.0).then_inc(e_cz, 1)
        g.wait_ge(e_cz, 1)
        if piece < 4:
            src, dst = T.cb[:, 0:QP], T.ident[:, QP * piece:QP * piece + QP]
            g.affine_select(src, src, [[-1, QP]], A.not_equal, 1.0, -QP * piece, 1).then_inc(e_c, 1)
            nc = 1
        elif piece == 4:
            src, dst = T.cb[:], T.R[:]
            for gi in range(3):
                ap = T.cb[QP * gi:QP * gi + QP, 0:3 * SLOT]
                g.affine_select(ap, ap, [[0, 3], [-1, SLOT]], A.not_equal, 1.0, 0, 1).then_inc(e_c, 1)
            nc = 3
        elif piece == 5:
            src, dst = T.cb[:, 0:QP], T.Sel[:]
            for s in range(3):
                g.affine_select(src, src, [[-1, QP]], A.not_equal, 1.0, -SLOT * s, 1).then_inc(e_c, 1)
                g.wait_ge(e_c, s + 1)
            nc = 3
        else:
            src, dst = T.pm[:], T.pm[:]
            g.affine_select(src, src, [[0, 4], [-SLOT, 3]], A.is_ge, BIG, 0, 1).then_inc(e_c, 1)
            g.wait_ge(e_c, 1)
            g.affine_select(src, src, [[0, 4], [SLOT, 3]], A.is_ge, BIG, SLOT - 1, -1).then_inc(e_c, 1)
            nc = 2
        g.wait_ge(e_c, nc)
        fused([tr(src, [dst], [c0], off, S.cst)])
        e_z, e_one, e_id, e_R = ev(), ev(), ev(), ev()
        DVE.memset(T.R[:], 0.0).then_inc(e_z, 1)
        ACT.wait_ge(e_z, 1)
        ACT.activation(T.ones[:], T.R[:], F.Exp).then_inc(e_one, 1)
        g.wait_ge(e_one, 1)
        g.affine_select(T.ident[:], T.ones[:], [[-1, 128]], A.is_equal, 0.0, 0, 1).then_inc(e_id, 1)
        DVE.wait_ge(e_z, 1)
        DVE.wait_ge(e_id, 1)
        nR = 0
        for gi in range(G):
            p0 = QP * gi
            for s in range(3):
                DVE.tensor_copy(T.R[p0:p0 + QP, SLOT * s:SLOT * s + QP],
                                T.ident[p0:p0 + QP, p0:p0 + QP]).then_inc(e_R, 1)
                nR += 1
        PE.wait_ge(e_id, 1)
        PE.wait_ge(e_R, nR)
        DVE.wait_ge(S.mk, len(on))

    dcs, dsts = [], []
    for t in carry:
        c, gi, _n = where[(t, j)]
        dcs.append(c)
        dsts.append(T.qs[:, QP * gi:QP * gi + QP])
    if is_rank:
        g.wait_ge(e_land, 1)
        g.wait_ge(S.qdl, 16)
        fused([tr(T.qd[:], [T.qd[:] for _ in helpers], helpers, hi, S.qdin),
               tr(T.qd[:], dsts, dcs, off, S.qin)])
        for buf, sem in ((T.ks, S.kin), (T.vs, S.vin)):
            g.wait_ge(sem, 16)
            fused([tr(buf[:], [buf[:] for _ in helpers], helpers, on, sem)])
    else:
        g.wait_ge(S.qdin, len(hi))
        fused([tr(T.qd[:], dsts, dcs, off, S.qin)])

    e_S, e_M, e_P, e_X, e_T0, e_T1, e_C0, e_C1, e_ST, e_O = [ev() for _ in range(10)]
    e_own, e_msg = ev(), ev()
    mask = T.maskR if is_rank else T.maskG
    if is_rank:
        PE.wait_ge(S.qown, 16)
    PE.wait_ge(S.qin, len(off) * len(guests))
    PE.wait_ge(S.kin, len(on))
    PE.matmul(T.pS[0:nq, 0:256], T.qs[:, 0:nq], T.ks[:], True, True).then_inc(e_S, 1)
    DVE.wait_ge(e_S, 1)
    DVE.tensor_reduce(T.negm[0:nq, :], T.pS[0:nq, 0:256], AX, A.max, negate=True).then_inc(e_M, 1)
    ACT.wait_ge(e_M, 1)
    ACT.activation(T.P[0:nq, :], T.pS[0:nq, 0:256], F.Exp, bias=T.negm[0:nq, :],
                   accum_out=T.lsum[0:nq, :]).then_inc(e_P, 1)
    DVE.wait_ge(e_M, 1)
    DVE.tensor_scalar(T.X[0:nq, 0:2 * G:2], mask[0:nq, 0:G], T.negm[0:nq, :], None, A.mult).then_inc(e_X, 1)
    DVE.wait_ge(e_P, 1)
    DVE.tensor_scalar(T.X[0:nq, 1:2 * G:2], mask[0:nq, 0:G], T.lsum[0:nq, :], None, A.mult).then_inc(e_X, 1)
    PE.wait_ge(e_M, 1)
    PE.wait_ge(e_P, 1)
    PE.transpose(T.pT0[0:128, 0:nq], T.P[0:nq, 0:128], T.ident[0:nq, 0:nq]).then_inc(e_T0, 1)
    PE.transpose(T.pT1[0:128, 0:nq], T.P[0:nq, 128:256], T.ident[0:nq, 0:nq]).then_inc(e_T1, 1)
    DVE.wait_ge(e_T0, 1)
    DVE.tensor_copy(T.PTs0[:, 0:nq], T.pT0[0:128, 0:nq]).then_inc(e_C0, 1)
    ACT.wait_ge(e_T1, 1)
    ACT.activation(T.PTs1[:, 0:nq], T.pT1[0:128, 0:nq], F.Copy).then_inc(e_C1, 1)
    PE.wait_ge(S.vin, len(on))
    PE.wait_ge(e_C0, 1)
    PE.matmul(T.pO[0:128, 0:nq], T.vs[:, 0:128], T.PTs0[:, 0:nq], True, False)
    PE.wait_ge(e_C1, 1)
    PE.matmul(T.pO[0:128, 0:nq], T.vs[:, 128:256], T.PTs1[:, 0:nq], False, True).then_inc(e_O, 1)
    PE.wait_ge(e_X, 2)
    PE.matmul(T.pST[0:128, 0:2 * G], T.R[0:nq, 0:128], T.X[0:nq, 0:2 * G], True, True).then_inc(e_ST, 1)

    def out_ap(gi, a, b):
        if served[gi] == j:
            at = SLOT * pos[(j, j)]
            return T.land[:, at + a:at + b], e_own
        return T.msg[:, SLOT * gi + a:SLOT * gi + b], e_msg

    ACT.wait_ge(e_ST, 1)
    order = [gi for gi in range(G) if served[gi] != j] + [gi for gi in range(G) if served[gi] == j]
    for gi in order:
        ap, e = out_ap(gi, QP, MSG)
        ACT.activation(ap, T.pST[0:128, 2 * gi:2 * gi + 2], F.Copy).then_inc(e, 1)
    DVE.wait_ge(e_O, 1)
    for gi in order:
        ap, e = out_ap(gi, 0, QP)
        DVE.tensor_copy(ap, T.pO[0:128, QP * gi:QP * gi + QP]).then_inc(e, 1)

    per = _per(len(guests), len(off))
    g.wait_ge(e_msg, 2 * len(guests))
    trs, at = [], 0
    for gi in range(G):
        r = served[gi]
        if r == j:
            continue
        sl = pos[(r, j)]
        trs.append(tr(T.msg[:, SLOT * gi:SLOT * gi + MSG], [T.land[:, SLOT * sl:SLOT * sl + MSG]], [cores[r]],
                      off[at:at + per], S["res%d" % (sl // 3)]))
        at += per
    fused(trs)
    g.wait_ge(S.sent, sent[0])
    if not is_rank:
        return

    tot = [0, 0, 0, 0]
    for t in range(n):
        if t != j:
            tot[pos[(j, t)] // 3] += _per(where[(t, j)][2], len(off))
    res = [S["res%d" % a] for a in range(4)]
    pT = [T.pT0, T.pT1, T.pT2, T.pT3]
    OTs = [T.OTs0, T.OTs1, T.OTs2, T.OTs3]
    Ws = [T.Ws0, T.Ws1]
    pYh = [T.pY, T.pS]
    W = 3 * SLOT
    H = 64
    e_TR = [ev() for _ in range(4)]
    e_sc = [ev() for _ in range(4)]
    e_W = [ev() for _ in range(4)]
    e_ws = [ev() for _ in range(2)]
    e_Y = [ev() for _ in range(2)]
    e_min, e_n01, e_n23, e_w12, e_wl, e_den, e_rden, e_ys = [ev() for _ in range(8)]
    nm12 = T.land[:, QP:12 * SLOT:SLOT]

    for a in range(4):
        PE.wait_ge(res[a], tot[a])
        if a == 0:
            PE.wait_ge(e_own, 2)
        PE.transpose(pT[a][0:W, 0:128], T.land[:, W * a:W * a + W], T.ident[:]).then_inc(e_TR[a], 1)
    DVE.wait_ge(res[0], tot[0])
    DVE.wait_ge(res[1], tot[1])
    DVE.wait_ge(e_own, 2)
    DVE.tensor_tensor(T.nmm[:, 0:6], T.land[:, QP:6 * SLOT:SLOT], T.pm[:, 0:6], A.add).then_inc(e_n01, 1)
    DVE.wait_ge(e_TR[0], 1)
    DVE.tensor_copy(OTs[0][0:W, :], pT[0][0:W, 0:128]).then_inc(e_sc[0], 1)
    ACT.wait_ge(e_TR[1], 1)
    ACT.activation(OTs[1][0:W, :], pT[1][0:W, 0:128], F.Copy).then_inc(e_sc[1], 1)
    DVE.wait_ge(res[2], tot[2])
    DVE.wait_ge(res[3], tot[3])
    DVE.tensor_reduce(T.minnm[:], nm12, AX, A.min).then_inc(e_min, 1)
    DVE.tensor_tensor(T.nmm[:, 6:12], T.land[:, 6 * SLOT + QP:12 * SLOT:SLOT], T.pm[:, 6:12], A.add).then_inc(e_n23, 1)

    def wexp(a):
        ACT.activation(T.wm[:, 3 * a:3 * a + 3], T.nmm[:, 3 * a:3 * a + 3], F.Exp, bias=T.minnm[:], scale=-1.0,
                       accum_out=T.wcol[:, a:a + 1]).then_inc(e_W[a], 1)

    for a in range(4):
        ACT.wait_ge(res[a], tot[a])
    ACT.wait_ge(e_own, 2)
    ACT.wait_ge(e_min, 1)
    ACT.wait_ge(e_n01, 1)
    wexp(0)
    ACT.activation(T.w12[0:QP, :], T.land[0:QP, QP:12 * SLOT:SLOT], F.Exp, bias=T.minnm[0:QP, :],
                   scale=-1.0).then_inc(e_w12, 1)
    wexp(1)
    ACT.wait_ge(e_n23, 1)
    wexp(2)
    wexp(3)
    for a in (0, 1):
        DVE.wait_ge(e_W[a], 1)
        DVE.tensor_scalar(Ws[a][0:W, :], T.Sel[0:W, :], T.wcol[0:W, a:a + 1], None, A.mult).then_inc(e_ws[a], 1)
    for a in (2, 3):
        ACT.wait_ge(e_W[a], 1)
        ACT.wait_ge(e_TR[a], 1)
        ACT.activation(OTs[a][0:W, :], pT[a][0:W, 0:128], F.Copy, scale=T.wcol[0:W, a:a + 1]).then_inc(e_sc[a], 1)
    DVE.wait_ge(e_w12, 1)
    DVE.tensor_tensor(T.wl[0:QP, :], T.w12[0:QP, :], T.land[0:QP, QP + 1:12 * SLOT:SLOT], A.mult).then_inc(e_wl, 1)
    DVE.wait_ge(e_wl, 1)
    DVE.tensor_reduce(T.den[0:QP, :], T.wl[0:QP, :], AX, A.add).then_inc(e_den, 1)
    DVE.wait_ge(e_den, 1)
    DVE.reciprocal(T.rden[0:QP, :], T.den[0:QP, :]).then_inc(e_rden, 1)
    for a in range(4):
        PE.wait_ge(e_sc[a], 1)
        if a < 2:
            PE.wait_ge(e_ws[a], 1)
            lhs = Ws[a][0:W, :]
        else:
            lhs = T.Sel[0:W, :]
        for h in range(2):
            mm = PE.matmul(pYh[h][0:QP, 0:H], lhs, OTs[a][0:W, H * h:H * h + H], a == 0, a == 3)
            if a == 3:
                mm.then_inc(e_Y[h], 1)
    DVE.wait_ge(e_rden, 1)
    DVE.wait_ge(e_Y[0], 1)
    DVE.tensor_scalar(T.ysb[0:QP, 0:H], pYh[0][0:QP, 0:H], T.rden[0:QP, :], None, A.mult).then_inc(e_ys, 1)
    ACT.wait_ge(e_rden, 1)
    ACT.wait_ge(e_Y[1], 1)
    ACT.activation(T.ysb[0:QP, H:2 * H], pYh[1][0:QP, 0:H], F.Copy, scale=T.rden[0:QP, :]).then_inc(e_ys, 1)
    SP.wait_ge(e_ys, 2)
    SP.dma_start(T.y[:], T.ysb[0:QP, :]).then_inc(S.stored, 16)
    SP.wait_ge(S.stored, 16)
